import numpy as np
CORES = [0,1,2,3,4,5,6,7,128,129,130,131,132,133,134,135,256,257,258,259,260,261,262,263,384,385,386,387,388,389,390,391]
N = 32
H = 1
ROWS, COLS = 4, 8
PERIODIC = True
def setup_inputs(rng):
    return {"x": rng.standard_normal((N, 128, 128), dtype=np.float32)}
def reference(x):
    W = x.shape[2]
    y = np.zeros((N, 4, 128, H), x.dtype)
    for r in range(N):
        i, j = divmod(r, COLS)
        for k, (di, dj, cols) in enumerate([(-1, 0, slice(W - H, W)), (1, 0, slice(0, H)), (0, -1, slice(W - H, W)), (0, 1, slice(0, H))]):
            a, b = i + di, j + dj
            if PERIODIC:
                a, b = a % ROWS, b % COLS
            if 0 <= a < ROWS and 0 <= b < COLS:
                y[r][k] = x[a * COLS + b][:, cols]
    return {"y": y}

from concourse.bass import DstId, RemoteDMATransfer

ROWS, COLS = 4, 8

SCRATCH = {
    "edge": ("dram", [2, 128, 1], "float32"),
    "land": ("dram", [4, 128, 1], "float32"),
}
SEMAPHORES = ["loaded", "sent", "arrived", "stored"]

ENG = 4
MASKS = (0x000F, 0x00F0, 0x0F00, 0xF000)


def rank_program(g, core, T, topo):
    rank = T.rank_of(core)
    if rank is None:
        return
    i, j = divmod(rank, COLS)
    W = T.x.shape[1]

    g.dma_start(T.edge[0], T.x[:, 0:1], allow_slow_non_contiguous=True).then_inc(T.sem.loaded, 16)
    g.dma_start(T.edge[1], T.x[:, W - 1:W], allow_slow_non_contiguous=True).then_inc(T.sem.loaded, 16)
    g.wait_ge(T.sem.loaded, 32)

    sends = (
        (((i + 1) % ROWS) * COLS + j, 0, 1),
        (((i - 1) % ROWS) * COLS + j, 1, 0),
        (i * COLS + (j + 1) % COLS, 2, 1),
        (i * COLS + (j - 1) % COLS, 3, 0),
    )
    transfers = []
    for (nb, slot, col), mask in zip(sends, MASKS):
        dst = T.cores[nb]
        rid, pid = topo.addr(dst, core)
        transfers.append(RemoteDMATransfer(dst_ids=[DstId(rid=rid, pnc=pid)], dma_engine_mask=mask,
                                           remote_sem=T.sem.arrived, src=T.edge[col], dst=T.land[slot]))
    g.remote_dma_fused(transfers, local_sem=T.sem.sent)

    g.wait_ge(T.sem.arrived, 4 * ENG)
    g.dma_start(T.y[:], T.land[:]).then_inc(T.sem.stored, 16)
    g.wait_ge(T.sem.sent, 4 * ENG)
    g.wait_ge(T.sem.stored, 16)
